import numpy as np
import ml_dtypes


def mxq(x, axis, fmt="e4m3"):
    dtype, down = {"e4m3": (ml_dtypes.float8_e4m3fn, 7), "e5m2": (ml_dtypes.float8_e5m2, 14)}[fmt]
    v = np.moveaxis(np.asarray(x, np.float32).astype(ml_dtypes.bfloat16).astype(np.float64), axis, -1)
    blocks = v.reshape(v.shape[:-1] + (-1, 32))
    amax = np.abs(blocks).max(-1, keepdims=True)
    byte = np.maximum(np.where(amax > 0, np.frexp(amax)[1] - 1 + 127, 0) - down, 1)
    scale = np.exp2(byte - 127.0)
    codes = (blocks / scale).astype(np.float32).astype(dtype).astype(np.float64)
    return np.moveaxis((codes * scale).reshape(v.shape), -1, axis)


WIDE = False


def mx_kscale(k):
    if not WIDE:
        return np.ones(k)
    levels = np.array([10, -10, 5, -5, 0])
    if k % 512:
        return np.exp2(np.random.permutation(np.resize(levels, k // 32))).repeat(32)
    a = np.empty((k // 512, 16))
    for p in range(k // 512):
        a[p, :8] = np.random.permutation(np.resize(levels, 8))
        for g in range(8):
            far = levels[np.abs(levels - a[p, g]) >= 10]
            a[p, g + 8] = far[np.random.randint(len(far))]
    return np.exp2(a.ravel()).repeat(32)


def f64(x):
    return np.asarray(x).astype(np.float64)


def striped8(idx):
    return np.asarray(idx).reshape(8, -1, 16).transpose(0, 2, 1).reshape(128, -1).astype(np.uint16)


def unstriped8(offs):
    return offs.reshape(8, 16, -1).transpose(0, 2, 1).reshape(8, -1).astype(np.int64)


def pick8(x, idx, run):
    r = np.arange(len(x))
    return x[r[:, None], idx[r % (8 * run) // run]]


E2M1 = np.array([0.0, 0.5, 1.0, 1.5, 2.0, 3.0, 4.0, 6.0, -0.0, -0.5, -1.0, -1.5, -2.0, -3.0, -4.0, -6.0])


def pack_weight(w, fmt):
    k, n = w.shape
    w = f64(np.asarray(w, np.float32).astype(ml_dtypes.bfloat16)).reshape(k // 32, 32, n)
    amax = np.abs(w).max(1)
    if fmt == "e4m3":
        byte = np.frexp(amax)[1] - 1 + 127 - 7
    else:
        mant, ex = np.frexp(amax / 6.0)
        byte = np.where(mant > 0.5, ex, ex - 1) + 127
    byte = np.clip(np.where(amax > 0, byte, 1), 1, 254)
    scaled = (w * np.exp2(127.0 - byte)[:, None, :]).reshape(k, n).astype(np.float32)
    by_word = np.ascontiguousarray(scaled.reshape(k // 512, 128, 4, n).transpose(0, 1, 3, 2))
    if fmt == "e4m3":
        words = by_word.astype(ml_dtypes.float8_e4m3fn).view(np.uint8)
    else:
        c = by_word.astype(ml_dtypes.float4_e2m1fn).view(np.uint8) & 0xF
        words = (c[..., 0::2] | (c[..., 1::2] << 4)).reshape(k // 512, 128, 2 * n)
    return np.ascontiguousarray(words), np.ascontiguousarray(byte.astype(np.uint8).reshape(k // 512, 16, n))


def unpack_weight(words, scales, fmt):
    g, _, n = scales.shape
    words = np.ascontiguousarray(words).reshape(g, 128, n, -1)
    if fmt == "e4m3":
        vals = words.view(ml_dtypes.float8_e4m3fn).astype(np.float64)
    else:
        nib = np.empty((g, 128, n, 4), np.uint8)
        nib[..., 0::2] = words & 0xF
        nib[..., 1::2] = words >> 4
        vals = E2M1[nib]
    vals = vals * np.repeat(np.exp2(scales.astype(np.float64) - 127.0), 8, axis=1)[..., None]
    return vals.transpose(0, 1, 3, 2).reshape(g * 512, n)


K, T, J, N, L = 512, 512, 512, 512, 512


def setup_inputs():
    n = np.random.standard_normal
    idx = np.stack([np.random.randint(0, T, J) for _ in range(8)])
    fk = mx_kscale(K)
    fl = mx_kscale(L)
    xtp = pack_weight(n((K, T)) / fk[:, None], "e4m3")
    wp = pack_weight(n((K, N)) * 1 / np.sqrt(K) * fk[:, None], "e2m1")
    wip = pack_weight(n((L, N)) * 1 / np.sqrt(L) * fl[:, None], "e4m3")
    return {
        "xt_words": xtp[0],
        "xt_scales": xtp[1],
        "w_words": wp[0],
        "w_scales": wp[1],
        "xi": (n((L, J)) / fl[:, None]).astype(np.float32),
        "wi_words": wip[0],
        "wi_scales": wip[1],
        "offs": striped8(idx),
    }


def reference(xt_words, xt_scales, w_words, w_scales, xi, wi_words, wi_scales, offs):
    idx = unstriped8(offs)
    xtu = unpack_weight(xt_words, xt_scales, "e4m3")
    wu = unpack_weight(w_words, w_scales, "e2m1")
    wiu = unpack_weight(wi_words, wi_scales, "e4m3")
    z = wu.T @ xtu
    u = pick8(z, idx, 64)
    xiq = mxq(f64(xi), 0, "e4m3")
    q = wiu.T @ xiq
    y = u * 1.0 / (np.max(np.abs(u), axis=1, keepdims=True) + 0.5) + 0.3 * q
    return y

@@ -1,0 +1,163 @@
+from contextlib import ExitStack
+
+import concourse.mybir as mybir
+
+K, T, J, N, L = 512, 512, 512, 512, 512
+FLOPS = 2 * K * N * T + 2 * L * N * J
+
+F32 = mybir.dt.float32
+BF16 = mybir.dt.bfloat16
+I32 = mybir.dt.int32
+U16 = mybir.dt.uint16
+U8 = mybir.dt.uint8
+FP8X4 = mybir.dt.float8_e4m3fn_x4
+FP4X4 = mybir.dt.float4_e2m1fn_x4
+ALU = mybir.AluOpType
+ACT = mybir.ActivationFunctionType
+P = 128
+TILES = 4
+RUN = 8
+CASTS = 4
+
+
+def tile_list_head_scaled_by_peak_kernel(tc, xt_words, xt_scales, w_words, w_scales, xi, wi_words, wi_scales, offs, out):
+    nc = tc.nc
+    with ExitStack() as ctx:
+        sb = ctx.enter_context(tc.tile_pool(name="sb", bufs=1))
+        ps = ctx.enter_context(tc.psum_pool(name="ps", bufs=1))
+
+        offsets = sb.tile([P, J // 16], U16, name="offsets")
+        w_raw = sb.tile([P, N // 2], I32, name="w_raw", align_bytes=64)
+        w_codes = sb.tile([P, 2 * N], U8, name="w_codes", align_bytes=64)
+        ws_raw = sb.tile([P, N // 4], I32, name="ws_raw", align_bytes=64)
+        w_sc = sb.tile([P, N], U8, name="w_sc", align_bytes=64)
+        xt_codes = sb.tile([P, T], I32, name="xt_codes", align_bytes=64)
+        xt_sc = sb.tile([P, T], U8, name="xt_sc", align_bytes=64)
+        wi_raw = sb.tile([P, N], I32, name="wi_raw", align_bytes=64)
+        wi_codes = sb.tile([P, N], I32, name="wi_codes", align_bytes=64)
+        wis_raw = sb.tile([P, N // 4], I32, name="wis_raw", align_bytes=64)
+        wi_sc = sb.tile([P, N], U8, name="wi_sc", align_bytes=64)
+        xi_raw = sb.tile([P, 4, J], F32, name="xi_raw", align_bytes=64)
+        u_all = sb.tile([P, 5 * J], F32, name="u_all", align_bytes=64)
+        xi_bf = u_all[:, 3 * J :].bitcast(BF16)
+        xi_codes = sb.tile([P, J], I32, name="xi_codes", align_bytes=64)
+        xi_sc = sb.tile([P, J], U8, name="xi_sc", align_bytes=64)
+        peak = sb.tile([P, TILES], F32, name="peak")
+        den = sb.tile([P, TILES], F32, name="den")
+        inv = sb.tile([P, TILES], F32, name="inv")
+
+        def load_scales(plane, scales):
+            rows = scales[0].bitcast(I32)
+            for q in range(4):
+                queue = nc.sync if q % 2 == 0 else nc.scalar
+                queue.dma_start(
+                    out=plane[32 * q : 32 * (q + 1), :],
+                    in_=rows[4 * q : 4 * q + 4, :].unsqueeze(0).to_broadcast([8, 4, N // 4]),
+                )
+
+        def deal(engine, dst, src, words):
+            engine.tensor_copy(
+                out=dst.rearrange("p (i g e) -> p i g e", i=TILES, e=words),
+                in_=src.rearrange("p (g i e) -> p i g e", i=TILES, e=words),
+            )
+
+        load_scales(ws_raw[:], w_scales)
+        nc.sync.dma_start(out=w_raw[:], in_=w_words[0].bitcast(I32))
+        nc.scalar.dma_start(out=xt_codes[:], in_=xt_words[0].rearrange("p n t -> p (n t)").bitcast(I32))
+        load_scales(xt_sc[:].bitcast(I32), xt_scales)
+        nc.sync.dma_start(offsets[:], offs)
+        nc.sync.dma_start(out=xi_raw[:], in_=xi.rearrange("(p t) j -> p t j", t=4))
+        nc.sync.dma_start(out=wi_raw[:], in_=wi_words[0].rearrange("p n t -> p (n t)").bitcast(I32))
+        wis_rows = wi_scales[0].bitcast(I32)
+        for q in range(4):
+            nc.sync.dma_start(
+                out=wis_raw[32 * q : 32 * (q + 1), :],
+                in_=wis_rows[4 * q : 4 * q + 4, :].unsqueeze(0).to_broadcast([8, 4, N // 4]),
+            )
+
+        deal(nc.vector, w_sc[:].bitcast(I32), ws_raw[:], RUN // 4)
+        deal(nc.vector, w_codes[:].bitcast(I32), w_raw[:], RUN // 2)
+
+        z = [sb.tile([P, T], F32, name="z%d" % i) for i in range(TILES)]
+        t = [sb.tile([P, J], F32, name="t%d" % i) for i in range(TILES)]
+        y = [sb.tile([P, J], F32, name="y%d" % i) for i in range(TILES)]
+
+        def z_product(i, a, b, tag):
+            bank = ps.tile([P, b - a], F32, name="z_bank", tag=tag)
+            nc.tensor.matmul_mx(
+                out=bank[:],
+                lhsT=w_codes[:, 2 * P * i : 2 * P * (i + 1)].bitcast(FP4X4),
+                lhsT_scale=w_sc[:, P * i : P * (i + 1)],
+                rhs=xt_codes[:, a:b].bitcast(FP8X4),
+                rhs_scale=xt_sc[:, a:b],
+                start=True,
+                stop=True,
+            )
+            return bank
+
+        nc.scalar.activation(out=z[0][:, : T // 2], in_=z_product(0, 0, T // 2, "b0")[:], func=ACT.Copy)
+        nc.vector.tensor_copy(out=z[0][:, T // 2 :], in_=z_product(0, T // 2, T, "b4")[:])
+        for i in range(1, TILES):
+            nc.scalar.activation(out=z[i][:], in_=z_product(i, 0, T, "b%d" % i)[:], func=ACT.Copy)
+
+        u = [u_all[:, i * J : (i + 1) * J] for i in range(TILES)]
+
+        def look_up(i):
+            for h in range(2):
+                nc.vector.tensor_copy(
+                    out=u[i][:, h * (J // 2) : (h + 1) * (J // 2)],
+                    in_=z[i][:].indirect(offsets[:, h * (J // 32) : (h + 1) * (J // 32)]),
+                )
+
+        def find_peaks(a, b):
+            nc.vector.tensor_reduce(
+                out=peak[:, a:b],
+                in_=u_all[:, a * J : b * J].rearrange("p (i j) -> p i j", j=J),
+                axis=mybir.AxisListType.X,
+                op=ALU.max,
+                apply_absolute_value=True,
+            )
+
+        def invert(a, b):
+            nc.vector.tensor_scalar(out=den[:, a:b], in0=peak[:, a:b], scalar1=0.5, scalar2=None, op0=ALU.add)
+            nc.vector.reciprocal(out=inv[:, a:b], in_=den[:, a:b])
+
+        rows = out.rearrange("(g i b) j -> i g b j", i=TILES, b=RUN)
+
+        def finish(i, a, b):
+            nc.vector.scalar_tensor_tensor(out=y[i][:, a:b], in0=u[i][:, a:b], scalar=inv[:, i : i + 1], in1=t[i][:, a:b], op0=ALU.mult, op1=ALU.add)
+            nc.sync.dma_start(out=rows[i][:, :, a:b], in_=y[i][:, a:b])
+
+        look_up(0)
+        width = J // CASTS
+        for c in range(CASTS):
+            nc.scalar.copy(
+                out=xi_bf[:, 4 * width * c : 4 * width * (c + 1)].rearrange("p (c i t) -> p c t i", i=4, t=4),
+                in_=xi_raw[:, :, width * c : width * (c + 1)].rearrange("p t (c i) -> p c t i", i=4),
+            )
+        look_up(1)
+        find_peaks(0, 2)
+        deal(nc.vector, wi_codes[:], wi_raw[:], RUN)
+        deal(nc.vector, wi_sc[:].bitcast(I32), wis_raw[:], RUN // 4)
+        look_up(2)
+        nc.vector.quantize_mx(out=xi_codes[:].bitcast(FP8X4), scales=xi_sc[:], in_=xi_bf)
+        for i in range(TILES):
+            bank = ps.tile([P, J], F32, name="q_bank", tag="b%d" % (4 + i))
+            nc.tensor.matmul_mx(
+                out=bank[:],
+                lhsT=wi_codes[:, P * i : P * (i + 1)].bitcast(FP8X4),
+                lhsT_scale=wi_sc[:, P * i : P * (i + 1)],
+                rhs=xi_codes[:].bitcast(FP8X4),
+                rhs_scale=xi_sc[:],
+                start=True,
+                stop=True,
+            )
+            nc.scalar.activation(out=t[i][:], in_=bank[:], func=ACT.Copy, scale=0.3)
+        invert(0, 2)
+        look_up(3)
+        find_peaks(2, 4)
+        invert(2, 4)
+        for i in range(TILES - 1):
+            finish(i, 0, J)
+        finish(3, 0, J // 2)
+        finish(3, J // 2, J)

@@ -34,55 +34,50 @@ def tile_list_head_scaled_by_peak_kernel(tc, xt_words, xt_scales, w_words, w_sca
         xt_codes = sb.tile([P, T], I32, name="xt_codes", align_bytes=64)
         xt_sc = sb.tile([P, T], U8, name="xt_sc", align_bytes=64)
         wi_raw = sb.tile([P, N], I32, name="wi_raw", align_bytes=64)
-        wi_codes = sb.tile([P, N], I32, name="wi_codes", align_bytes=64)
-        wis_raw = sb.tile([P, N // 4], I32, name="wis_raw", align_bytes=64)
-        wi_sc = sb.tile([P, N], U8, name="wi_sc", align_bytes=64)
-        xi_raw = sb.tile([P, 4, J], F32, name="xi_raw", align_bytes=64)
-        u_all = sb.tile([P, 5 * J], F32, name="u_all", align_bytes=64)
-        xi_bf = u_all[:, 3 * J :].bitcast(BF16)
+        wis_raw = sb.tile([P, N // 4], I32, name="wis_raw", tag="planes", align_bytes=64)
+        xi_raw = sb.tile([P, 4, J], F32, name="xi_raw", tag="xi", align_bytes=64)
         xi_codes = sb.tile([P, J], I32, name="xi_codes", align_bytes=64)
-        xi_sc = sb.tile([P, J], U8, name="xi_sc", align_bytes=64)
+        u_all = sb.tile([P, TILES * J], F32, name="u_all", align_bytes=64)
+        u = [u_all[:, i * J : (i + 1) * J] for i in range(TILES)]
+        xi_bf = u_all[:, 2 * J :].bitcast(BF16)
         peak = sb.tile([P, TILES], F32, name="peak")
         den = sb.tile([P, TILES], F32, name="den")
         inv = sb.tile([P, TILES], F32, name="inv")
+        z = [sb.tile([P, 2 * T], F32, name="z", tag="z%d" % i, align_bytes=64) for i in range(TILES)]
+        t = [sb.tile([P, J], F32, name="t%d" % i) for i in range(TILES)]
+        y = [sb.tile([P, J], F32, name="y%d" % i) for i in range(TILES)]
 
-        def load_scales(plane, scales):
-            rows = scales[0].bitcast(I32)
-            for q in range(4):
-                queue = nc.sync if q % 2 == 0 else nc.scalar
-                queue.dma_start(
-                    out=plane[32 * q : 32 * (q + 1), :],
-                    in_=rows[4 * q : 4 * q + 4, :].unsqueeze(0).to_broadcast([8, 4, N // 4]),
-                )
+        def load_scale_rows(queue, plane, scales, q):
+            rows = scales[0].bitcast(I32)[4 * q : 4 * q + 4, :]
+            queue.dma_start(out=plane[32 * q : 32 * (q + 1), :], in_=rows.unsqueeze(0).to_broadcast([8, 4, N // 4]))
 
-        def deal(engine, dst, src, words):
-            engine.tensor_copy(
+        def deal(dst, src, words):
+            nc.vector.tensor_copy(
                 out=dst.rearrange("p (i g e) -> p i g e", i=TILES, e=words),
                 in_=src.rearrange("p (g i e) -> p i g e", i=TILES, e=words),
             )
 
-        load_scales(ws_raw[:], w_scales)
+        for i in range(TILES):
+            nc.vector.memset(z[i][:, T:], 0.0)
+
+        for q in range(4):
+            load_scale_rows(nc.sync if q % 2 == 0 else nc.scalar, ws_raw[:], w_scales, q)
         nc.sync.dma_start(out=w_raw[:], in_=w_words[0].bitcast(I32))
         nc.scalar.dma_start(out=xt_codes[:], in_=xt_words[0].rearrange("p n t -> p (n t)").bitcast(I32))
-        load_scales(xt_sc[:].bitcast(I32), xt_scales)
-        nc.sync.dma_start(offsets[:], offs)
-        nc.sync.dma_start(out=xi_raw[:], in_=xi.rearrange("(p t) j -> p t j", t=4))
-        nc.sync.dma_start(out=wi_raw[:], in_=wi_words[0].rearrange("p n t -> p (n t)").bitcast(I32))
-        wis_rows = wi_scales[0].bitcast(I32)
         for q in range(4):
-            nc.sync.dma_start(
-                out=wis_raw[32 * q : 32 * (q + 1), :],
-                in_=wis_rows[4 * q : 4 * q + 4, :].unsqueeze(0).to_broadcast([8, 4, N // 4]),
-            )
+            load_scale_rows(nc.sync if q % 2 == 0 else nc.scalar, xt_sc[:].bitcast(I32), xt_scales, q)
+        nc.sync.dma_start(offsets[:], offs)
+        nc.scalar.dma_start(out=wi_raw[:], in_=wi_words[0].rearrange("p n t -> p (n t)").bitcast(I32))
+        nc.sync.dma_start(out=xi_raw[:], in_=xi.rearrange("(p t) j -> p t j", t=4))
+        for q in range(4):
+            load_scale_rows(nc.sync, wis_raw[:], wi_scales, q)
 
-        deal(nc.vector, w_sc[:].bitcast(I32), ws_raw[:], RUN // 4)
-        deal(nc.vector, w_codes[:].bitcast(I32), w_raw[:], RUN // 2)
+        deal(w_sc[:].bitcast(I32), ws_raw[:], RUN // 4)
+        deal(w_codes[:].bitcast(I32), w_raw[:], RUN // 2)
+        wi_codes = sb.tile([P, N], I32, name="wi_codes", align_bytes=64)
+        deal(wi_codes[:], wi_raw[:], RUN)
 
-        z = [sb.tile([P, T], F32, name="z%d" % i) for i in range(TILES)]
-        t = [sb.tile([P, J], F32, name="t%d" % i) for i in range(TILES)]
-        y = [sb.tile([P, J], F32, name="y%d" % i) for i in range(TILES)]
-
-        def z_product(i, a, b, tag):
+        def z_product(i, a, b, tag, copy):
             bank = ps.tile([P, b - a], F32, name="z_bank", tag=tag)
             nc.tensor.matmul_mx(
                 out=bank[:],
@@ -93,21 +88,24 @@ def tile_list_head_scaled_by_peak_kernel(tc, xt_words, xt_scales, w_words, w_sca
                 start=True,
                 stop=True,
             )
-            return bank
+            copy(z[i][:, a:b], bank[:])
 
-        nc.scalar.activation(out=z[0][:, : T // 2], in_=z_product(0, 0, T // 2, "b0")[:], func=ACT.Copy)
-        nc.vector.tensor_copy(out=z[0][:, T // 2 :], in_=z_product(0, T // 2, T, "b4")[:])
+        def scalar_copy(dst, src):
+            nc.scalar.activation(out=dst, in_=src, func=ACT.Copy)
+
+        for c in range(4):
+            z_product(0, c * T // 4, (c + 1) * T // 4, "b%d" % (4 + c), scalar_copy if c % 2 == 0 else nc.vector.tensor_copy)
         for i in range(1, TILES):
-            nc.scalar.activation(out=z[i][:], in_=z_product(i, 0, T, "b%d" % i)[:], func=ACT.Copy)
-
-        u = [u_all[:, i * J : (i + 1) * J] for i in range(TILES)]
+            z_product(i, 0, T, "b%d" % i, scalar_copy)
+        width = J // CASTS
+        for c in range(CASTS):
+            nc.scalar.copy(
+                out=xi_bf[:, 4 * width * c : 4 * width * (c + 1)].rearrange("p (c i t) -> p c t i", i=4, t=4),
+                in_=xi_raw[:, :, width * c : width * (c + 1)].rearrange("p t (c i) -> p c t i", i=4),
+            )
 
         def look_up(i):
-            for h in range(2):
-                nc.vector.tensor_copy(
-                    out=u[i][:, h * (J // 2) : (h + 1) * (J // 2)],
-                    in_=z[i][:].indirect(offsets[:, h * (J // 32) : (h + 1) * (J // 32)]),
-                )
+            nc.vector.tensor_copy(out=u[i], in_=z[i][:].indirect(offsets[:]))
 
         def find_peaks(a, b):
             nc.vector.tensor_reduce(
@@ -129,19 +127,17 @@ def tile_list_head_scaled_by_peak_kernel(tc, xt_words, xt_scales, w_words, w_sca
             nc.sync.dma_start(out=rows[i][:, :, a:b], in_=y[i][:, a:b])
 
         look_up(0)
-        width = J // CASTS
-        for c in range(CASTS):
-            nc.scalar.copy(
-                out=xi_bf[:, 4 * width * c : 4 * width * (c + 1)].rearrange("p (c i t) -> p c t i", i=4, t=4),
-                in_=xi_raw[:, :, width * c : width * (c + 1)].rearrange("p t (c i) -> p c t i", i=4),
-            )
         look_up(1)
+        wi_sc = sb.tile([P, N], U8, name="wi_sc", tag="z1", align_bytes=64)
+        deal(wi_sc[:].bitcast(I32), wis_raw[:], RUN // 4)
         find_peaks(0, 2)
-        deal(nc.vector, wi_codes[:], wi_raw[:], RUN)
-        deal(nc.vector, wi_sc[:].bitcast(I32), wis_raw[:], RUN // 4)
-        look_up(2)
+        invert(0, 2)
+        xi_sc = sb.tile([P, J], U8, name="xi_sc", tag="planes", align_bytes=64)
         nc.vector.quantize_mx(out=xi_codes[:].bitcast(FP8X4), scales=xi_sc[:], in_=xi_bf)
-        for i in range(TILES):
+        scaled = sb.tile([P, 2, J], F32, name="scaled", tag="xi", align_bytes=64)
+        for i in range(2):
+            nc.scalar.activation(out=scaled[:, i, :], in_=u[i], func=ACT.Copy, scale=inv[:, i : i + 1])
+        for i in (2, 0, 1, 3):
             bank = ps.tile([P, J], F32, name="q_bank", tag="b%d" % (4 + i))
             nc.tensor.matmul_mx(
                 out=bank[:],
@@ -153,11 +149,16 @@ def tile_list_head_scaled_by_peak_kernel(tc, xt_words, xt_scales, w_words, w_sca
                 stop=True,
             )
             nc.scalar.activation(out=t[i][:], in_=bank[:], func=ACT.Copy, scale=0.3)
-        invert(0, 2)
+            if i < 2:
+                nc.gpsimd.tensor_tensor(out=y[i][:], in0=scaled[:, i, :], in1=t[i][:], op=ALU.add)
+                nc.sync.dma_start(out=rows[i], in_=y[i][:])
+        look_up(2)
         look_up(3)
-        find_peaks(2, 4)
-        invert(2, 4)
-        for i in range(TILES - 1):
+        find_peaks(2, 3)
+        find_peaks(3, 4)
+        invert(2, 3)
+        invert(3, 4)
+        for i in range(2, TILES - 1):
             finish(i, 0, J)
         finish(3, 0, J // 2)
         finish(3, J // 2, J)

@@ -35,7 +35,7 @@ def tile_list_head_scaled_by_peak_kernel(tc, xt_words, xt_scales, w_words, w_sca
         xt_sc = sb.tile([P, T], U8, name="xt_sc", align_bytes=64)
         wi_raw = sb.tile([P, N], I32, name="wi_raw", align_bytes=64)
         wis_raw = sb.tile([P, N // 4], I32, name="wis_raw", tag="planes", align_bytes=64)
-        xi_raw = sb.tile([P, 4, J], F32, name="xi_raw", tag="xi", align_bytes=64)
+        xi_raw = [sb.tile([P, 4, J // 2], F32, name="xi_raw", tag="xi%d" % h, align_bytes=64) for h in range(2)]
         xi_codes = sb.tile([P, J], I32, name="xi_codes", align_bytes=64)
         u_all = sb.tile([P, TILES * J], F32, name="u_all", align_bytes=64)
         u = [u_all[:, i * J : (i + 1) * J] for i in range(TILES)]
@@ -68,9 +68,11 @@ def tile_list_head_scaled_by_peak_kernel(tc, xt_words, xt_scales, w_words, w_sca
             load_scale_rows(nc.sync if q % 2 == 0 else nc.scalar, xt_sc[:].bitcast(I32), xt_scales, q)
         nc.sync.dma_start(offsets[:], offs)
         nc.scalar.dma_start(out=wi_raw[:], in_=wi_words[0].rearrange("p n t -> p (n t)").bitcast(I32))
-        nc.sync.dma_start(out=xi_raw[:], in_=xi.rearrange("(p t) j -> p t j", t=4))
+        xi_rows = xi.rearrange("(p t) j -> p t j", t=4)
+        nc.sync.dma_start(out=xi_raw[0][:], in_=xi_rows[:, :, : J // 2])
         for q in range(4):
             load_scale_rows(nc.sync, wis_raw[:], wi_scales, q)
+        nc.sync.dma_start(out=xi_raw[1][:], in_=xi_rows[:, :, J // 2 :])
 
         deal(w_sc[:].bitcast(I32), ws_raw[:], RUN // 4)
         deal(w_codes[:].bitcast(I32), w_raw[:], RUN // 2)
@@ -101,7 +103,7 @@ def tile_list_head_scaled_by_peak_kernel(tc, xt_words, xt_scales, w_words, w_sca
         for c in range(CASTS):
             nc.scalar.copy(
                 out=xi_bf[:, 4 * width * c : 4 * width * (c + 1)].rearrange("p (c i t) -> p c t i", i=4, t=4),
-                in_=xi_raw[:, :, width * c : width * (c + 1)].rearrange("p t (c i) -> p c t i", i=4),
+                in_=xi_raw[c // 2][:, :, width * (c % 2) : width * (c % 2 + 1)].rearrange("p t (c i) -> p c t i", i=4),
             )
 
         def look_up(i):
@@ -134,10 +136,10 @@ def tile_list_head_scaled_by_peak_kernel(tc, xt_words, xt_scales, w_words, w_sca
         invert(0, 2)
         xi_sc = sb.tile([P, J], U8, name="xi_sc", tag="planes", align_bytes=64)
         nc.vector.quantize_mx(out=xi_codes[:].bitcast(FP8X4), scales=xi_sc[:], in_=xi_bf)
-        scaled = sb.tile([P, 2, J], F32, name="scaled", tag="xi", align_bytes=64)
+        scaled = sb.tile([P, 2, J], F32, name="scaled", tag="xi1", align_bytes=64)
         for i in range(2):
             nc.scalar.activation(out=scaled[:, i, :], in_=u[i], func=ACT.Copy, scale=inv[:, i : i + 1])
-        for i in (2, 0, 1, 3):
+        for i in range(TILES):
             bank = ps.tile([P, J], F32, name="q_bank", tag="b%d" % (4 + i))
             nc.tensor.matmul_mx(
                 out=bank[:],

from contextlib import ExitStack

import concourse.mybir as mybir

K, T, J, N, L = 512, 512, 512, 512, 512
FLOPS = 2 * K * N * T + 2 * L * N * J

F32 = mybir.dt.float32
BF16 = mybir.dt.bfloat16
I32 = mybir.dt.int32
U16 = mybir.dt.uint16
U8 = mybir.dt.uint8
FP8X4 = mybir.dt.float8_e4m3fn_x4
FP4X4 = mybir.dt.float4_e2m1fn_x4
ALU = mybir.AluOpType
ACT = mybir.ActivationFunctionType
P = 128
TILES = 4
RUN = 8
CASTS = 4


def tile_list_head_scaled_by_peak_kernel(tc, xt_words, xt_scales, w_words, w_scales, xi, wi_words, wi_scales, offs, out):
    nc = tc.nc
    with ExitStack() as ctx:
        sb = ctx.enter_context(tc.tile_pool(name="sb", bufs=1))
        ps = ctx.enter_context(tc.psum_pool(name="ps", bufs=1))

        offsets = sb.tile([P, J // 16], U16, name="offsets")
        w_raw = sb.tile([P, N // 2], I32, name="w_raw", align_bytes=64)
        w_codes = sb.tile([P, 2 * N], U8, name="w_codes", align_bytes=64)
        ws_raw = sb.tile([P, N // 4], I32, name="ws_raw", align_bytes=64)
        w_sc = sb.tile([P, N], U8, name="w_sc", align_bytes=64)
        xt_codes = sb.tile([P, T], I32, name="xt_codes", align_bytes=64)
        xt_sc = sb.tile([P, T], U8, name="xt_sc", align_bytes=64)
        wi_raw = sb.tile([P, N], I32, name="wi_raw", align_bytes=64)
        wis_raw = sb.tile([P, N // 4], I32, name="wis_raw", tag="planes", align_bytes=64)
        xi_raw = [sb.tile([P, 4, J // 2], F32, name="xi_raw", tag="xi%d" % h, align_bytes=64) for h in range(2)]
        xi_codes = sb.tile([P, J], I32, name="xi_codes", align_bytes=64)
        u_all = sb.tile([P, TILES * J], F32, name="u_all", align_bytes=64)
        u = [u_all[:, i * J : (i + 1) * J] for i in range(TILES)]
        xi_bf = u_all[:, 2 * J :].bitcast(BF16)
        peak = sb.tile([P, TILES], F32, name="peak")
        den = sb.tile([P, TILES], F32, name="den")
        inv = sb.tile([P, TILES], F32, name="inv")
        z = [sb.tile([P, 2 * T], F32, name="z", tag="z%d" % i, align_bytes=64) for i in range(TILES)]
        t = [sb.tile([P, J], F32, name="t%d" % i) for i in range(TILES)]
        y = [sb.tile([P, J], F32, name="y%d" % i) for i in range(TILES)]

        def load_scale_rows(queue, plane, scales, q):
            rows = scales[0].bitcast(I32)[4 * q : 4 * q + 4, :]
            queue.dma_start(out=plane[32 * q : 32 * (q + 1), :], in_=rows.unsqueeze(0).to_broadcast([8, 4, N // 4]))

        def deal(dst, src, words):
            nc.vector.tensor_copy(
                out=dst.rearrange("p (i g e) -> p i g e", i=TILES, e=words),
                in_=src.rearrange("p (g i e) -> p i g e", i=TILES, e=words),
            )

        for i in range(TILES):
            nc.vector.memset(z[i][:, T:], 0.0)

        for q in range(4):
            load_scale_rows(nc.sync if q % 2 == 0 else nc.scalar, ws_raw[:], w_scales, q)
        nc.sync.dma_start(out=w_raw[:], in_=w_words[0].bitcast(I32))
        nc.scalar.dma_start(out=xt_codes[:], in_=xt_words[0].rearrange("p n t -> p (n t)").bitcast(I32))
        for q in range(4):
            load_scale_rows(nc.sync if q % 2 == 0 else nc.scalar, xt_sc[:].bitcast(I32), xt_scales, q)
        nc.sync.dma_start(offsets[:], offs)
        nc.scalar.dma_start(out=wi_raw[:], in_=wi_words[0].rearrange("p n t -> p (n t)").bitcast(I32))
        xi_rows = xi.rearrange("(p t) j -> p t j", t=4)
        nc.sync.dma_start(out=xi_raw[0][:], in_=xi_rows[:, :, : J // 2])
        for q in range(4):
            load_scale_rows(nc.sync, wis_raw[:], wi_scales, q)
        nc.sync.dma_start(out=xi_raw[1][:], in_=xi_rows[:, :, J // 2 :])

        deal(w_sc[:].bitcast(I32), ws_raw[:], RUN // 4)
        deal(w_codes[:].bitcast(I32), w_raw[:], RUN // 2)
        wi_codes = sb.tile([P, N], I32, name="wi_codes", align_bytes=64)
        deal(wi_codes[:], wi_raw[:], RUN)

        def z_product(i, a, b, tag, copy):
            bank = ps.tile([P, b - a], F32, name="z_bank", tag=tag)
            nc.tensor.matmul_mx(
                out=bank[:],
                lhsT=w_codes[:, 2 * P * i : 2 * P * (i + 1)].bitcast(FP4X4),
                lhsT_scale=w_sc[:, P * i : P * (i + 1)],
                rhs=xt_codes[:, a:b].bitcast(FP8X4),
                rhs_scale=xt_sc[:, a:b],
                start=True,
                stop=True,
            )
            copy(z[i][:, a:b], bank[:])

        def scalar_copy(dst, src):
            nc.scalar.activation(out=dst, in_=src, func=ACT.Copy)

        for c in range(4):
            z_product(0, c * T // 4, (c + 1) * T // 4, "b%d" % (4 + c), scalar_copy if c % 2 == 0 else nc.vector.tensor_copy)
        for i in range(1, TILES):
            z_product(i, 0, T, "b%d" % i, scalar_copy)
        width = J // CASTS
        for c in range(CASTS):
            nc.scalar.copy(
                out=xi_bf[:, 4 * width * c : 4 * width * (c + 1)].rearrange("p (c i t) -> p c t i", i=4, t=4),
                in_=xi_raw[c // 2][:, :, width * (c % 2) : width * (c % 2 + 1)].rearrange("p t (c i) -> p c t i", i=4),
            )

        def look_up(i):
            nc.vector.tensor_copy(out=u[i], in_=z[i][:].indirect(offsets[:]))

        def find_peaks(a, b):
            nc.vector.tensor_reduce(
                out=peak[:, a:b],
                in_=u_all[:, a * J : b * J].rearrange("p (i j) -> p i j", j=J),
                axis=mybir.AxisListType.X,
                op=ALU.max,
                apply_absolute_value=True,
            )

        def invert(a, b):
            nc.vector.tensor_scalar(out=den[:, a:b], in0=peak[:, a:b], scalar1=0.5, scalar2=None, op0=ALU.add)
            nc.vector.reciprocal(out=inv[:, a:b], in_=den[:, a:b])

        rows = out.rearrange("(g i b) j -> i g b j", i=TILES, b=RUN)

        def finish(i, a, b):
            nc.vector.scalar_tensor_tensor(out=y[i][:, a:b], in0=u[i][:, a:b], scalar=inv[:, i : i + 1], in1=t[i][:, a:b], op0=ALU.mult, op1=ALU.add)
            nc.sync.dma_start(out=rows[i][:, :, a:b], in_=y[i][:, a:b])

        look_up(0)
        look_up(1)
        wi_sc = sb.tile([P, N], U8, name="wi_sc", tag="z1", align_bytes=64)
        deal(wi_sc[:].bitcast(I32), wis_raw[:], RUN // 4)
        find_peaks(0, 2)
        invert(0, 2)
        xi_sc = sb.tile([P, J], U8, name="xi_sc", tag="planes", align_bytes=64)
        nc.vector.quantize_mx(out=xi_codes[:].bitcast(FP8X4), scales=xi_sc[:], in_=xi_bf)
        scaled = sb.tile([P, 2, J], F32, name="scaled", tag="xi1", align_bytes=64)
        for i in range(2):
            nc.scalar.activation(out=scaled[:, i, :], in_=u[i], func=ACT.Copy, scale=inv[:, i : i + 1])
        for i in range(TILES):
            bank = ps.tile([P, J], F32, name="q_bank", tag="b%d" % (4 + i))
            nc.tensor.matmul_mx(
                out=bank[:],
                lhsT=wi_codes[:, P * i : P * (i + 1)].bitcast(FP8X4),
                lhsT_scale=wi_sc[:, P * i : P * (i + 1)],
                rhs=xi_codes[:].bitcast(FP8X4),
                rhs_scale=xi_sc[:],
                start=True,
                stop=True,
            )
            nc.scalar.activation(out=t[i][:], in_=bank[:], func=ACT.Copy, scale=0.3)
            if i < 2:
                nc.gpsimd.tensor_tensor(out=y[i][:], in0=scaled[:, i, :], in1=t[i][:], op=ALU.add)
                nc.sync.dma_start(out=rows[i], in_=y[i][:])
        look_up(2)
        look_up(3)
        find_peaks(2, 3)
        find_peaks(3, 4)
        invert(2, 3)
        invert(3, 4)
        for i in range(2, TILES - 1):
            finish(i, 0, J)
        finish(3, 0, J // 2)
        finish(3, J // 2, J)
